import numpy as np
import ml_dtypes


def mxq(x, axis, fmt="e4m3"):
    dtype, down = {"e4m3": (ml_dtypes.float8_e4m3fn, 7), "e5m2": (ml_dtypes.float8_e5m2, 14)}[fmt]
    v = np.moveaxis(np.asarray(x, np.float32).astype(ml_dtypes.bfloat16).astype(np.float64), axis, -1)
    blocks = v.reshape(v.shape[:-1] + (-1, 32))
    amax = np.abs(blocks).max(-1, keepdims=True)
    byte = np.maximum(np.where(amax > 0, np.frexp(amax)[1] - 1 + 127, 0) - down, 1)
    scale = np.exp2(byte - 127.0)
    codes = (blocks / scale).astype(np.float32).astype(dtype).astype(np.float64)
    return np.moveaxis((codes * scale).reshape(v.shape), -1, axis)


WIDE = False


def mx_kscale(k):
    if not WIDE:
        return np.ones(k)
    levels = np.array([10, -10, 5, -5, 0])
    if k % 512:
        return np.exp2(np.random.permutation(np.resize(levels, k // 32))).repeat(32)
    a = np.empty((k // 512, 16))
    for p in range(k // 512):
        a[p, :8] = np.random.permutation(np.resize(levels, 8))
        for g in range(8):
            far = levels[np.abs(levels - a[p, g]) >= 10]
            a[p, g + 8] = far[np.random.randint(len(far))]
    return np.exp2(a.ravel()).repeat(32)


def f64(x):
    return np.asarray(x).astype(np.float64)


def striped(idx):
    return np.tile(np.asarray(idx).reshape(-1, 16).T, (8, 1)).astype(np.uint16)


def unstriped(offs):
    return offs[:16].T.reshape(-1).astype(np.int64)


def striped8(idx):
    return np.asarray(idx).reshape(8, -1, 16).transpose(0, 2, 1).reshape(128, -1).astype(np.uint16)


def unstriped8(offs):
    return offs.reshape(8, 16, -1).transpose(0, 2, 1).reshape(8, -1).astype(np.int64)


def pick8(x, idx, run):
    r = np.arange(len(x))
    return x[r[:, None], idx[r % (8 * run) // run]]


E2M1 = np.array([0.0, 0.5, 1.0, 1.5, 2.0, 3.0, 4.0, 6.0, -0.0, -0.5, -1.0, -1.5, -2.0, -3.0, -4.0, -6.0])


def pack_weight(w, fmt):
    k, n = w.shape
    w = f64(np.asarray(w, np.float32).astype(ml_dtypes.bfloat16)).reshape(k // 32, 32, n)
    amax = np.abs(w).max(1)
    if fmt == "e4m3":
        byte = np.frexp(amax)[1] - 1 + 127 - 7
    else:
        mant, ex = np.frexp(amax / 6.0)
        byte = np.where(mant > 0.5, ex, ex - 1) + 127
    byte = np.clip(np.where(amax > 0, byte, 1), 1, 254)
    scaled = (w * np.exp2(127.0 - byte)[:, None, :]).reshape(k, n).astype(np.float32)
    by_word = np.ascontiguousarray(scaled.reshape(k // 512, 128, 4, n).transpose(0, 1, 3, 2))
    if fmt == "e4m3":
        words = by_word.astype(ml_dtypes.float8_e4m3fn).view(np.uint8)
    else:
        c = by_word.astype(ml_dtypes.float4_e2m1fn).view(np.uint8) & 0xF
        words = (c[..., 0::2] | (c[..., 1::2] << 4)).reshape(k // 512, 128, 2 * n)
    return np.ascontiguousarray(words), np.ascontiguousarray(byte.astype(np.uint8).reshape(k // 512, 16, n))


def unpack_weight(words, scales, fmt):
    g, _, n = scales.shape
    words = np.ascontiguousarray(words).reshape(g, 128, n, -1)
    if fmt == "e4m3":
        vals = words.view(ml_dtypes.float8_e4m3fn).astype(np.float64)
    else:
        nib = np.empty((g, 128, n, 4), np.uint8)
        nib[..., 0::2] = words & 0xF
        nib[..., 1::2] = words >> 4
        vals = E2M1[nib]
    vals = vals * np.repeat(np.exp2(scales.astype(np.float64) - 127.0), 8, axis=1)[..., None]
    return vals.transpose(0, 1, 3, 2).reshape(g * 512, n)


K, J, R, T, F, O, C, S, N, U = 512, 512, 512, 1024, 1024, 256, 512, 256, 256, 128


def setup_inputs():
    n = np.random.standard_normal
    idx = np.stack([np.random.permutation(T)[:J] for _ in range(8)])
    idx2 = np.random.permutation(F)[:R]
    idx3 = np.stack([np.random.permutation(J)[:S] for _ in range(8)])
    idx4 = np.stack([np.random.permutation(C)[:S] for _ in range(8)])
    idx5 = np.stack([np.random.permutation(C)[:O] for _ in range(8)])
    idx6 = np.stack([np.random.permutation(O)[:U] for _ in range(8)])
    idx7 = np.stack([np.random.permutation(O)[:U] for _ in range(8)])
    fk = mx_kscale(K)
    fr = mx_kscale(R)
    tr = np.ones(F)
    tr[idx2] = fr
    wtp = pack_weight(n((K, F)) * 1 / np.sqrt(K) / fk[:, None] * tr, "e4m3")
    wbp = pack_weight(n((R, N)) * 1 / np.sqrt(R) / fr[:, None], "e2m1")
    wop = pack_weight(n((R, N)) * 1 / np.sqrt(R) / fr[:, None], "e4m3")
    return {
        "ta": (np.random.randint(-7, 8, (K, T)).astype(np.float64)).astype(np.float32),
        "ga": ((np.random.randint(8, 25, (K, 1)) / 64.0) * fk[:, None]).astype(np.float32),
        "wt_words": wtp[0],
        "wt_scales": wtp[1],
        "sa": (np.random.uniform(0.5, 1.6, (R, 1))).astype(np.float32),
        "sb": (np.random.uniform(0.5, 1.6, (R, 1))).astype(np.float32),
        "wb_words": wbp[0],
        "wb_scales": wbp[1],
        "wo_words": wop[0],
        "wo_scales": wop[1],
        "so": (np.random.uniform(0.5, 1.6, (N, 1))).astype(np.float32),
        "sp": (np.random.uniform(0.5, 1.6, (N, 1))).astype(np.float32),
        "offs": striped8(idx),
        "offs2": striped(idx2),
        "offs3": striped8(idx3),
        "offs4": striped8(idx4),
        "offs5": striped8(idx5),
        "offs6": striped8(idx6),
        "offs7": striped8(idx7),
    }


def reference(ta, ga, wt_words, wt_scales, sa, sb, wb_words, wb_scales, wo_words, wo_scales, so, sp, offs, offs2, offs3, offs4, offs5, offs6, offs7):
    idx = unstriped8(offs)
    idx2 = unstriped(offs2)
    idx3 = unstriped8(offs3)
    idx4 = unstriped8(offs4)
    idx5 = unstriped8(offs5)
    idx6 = unstriped8(offs6)
    idx7 = unstriped8(offs7)
    wtu = unpack_weight(wt_words, wt_scales, "e4m3")
    wbu = unpack_weight(wb_words, wb_scales, "e2m1")
    wou = unpack_weight(wo_words, wo_scales, "e4m3")
    xc = pick8(f64(ta), idx, 64) * f64(ga)
    wtidx2g = wtu[:, idx2]
    xcq = mxq(xc, 0, "e4m3")
    a = wtidx2g.T @ xcq
    h1 = pick8(a, idx3, 64) * f64(sa)
    pw = np.zeros((R, C))
    pw[np.arange(R)[:, None], idx4[np.arange(R) % 512 // 64]] = h1
    g1 = np.maximum(pw, 0.0)
    hid = pick8(g1, idx5, 64) * f64(sb)
    hidq = mxq(hid, 0, "e4m3")
    p = wbu.T @ hidq
    q = wou.T @ hidq
    y = pick8(p, idx6, 16) * f64(so) - pick8(q, idx7, 16) * f64(sp)
    return y

@@ -1,0 +1,237 @@
+from contextlib import ExitStack
+
+import concourse.mybir as mybir
+
+K, J, R, T, F, O, C, S, N, U = 512, 512, 512, 1024, 1024, 256, 512, 256, 256, 128
+FLOPS = 2 * K * R * J + 2 * 2 * R * N * O
+
+F32 = mybir.dt.float32
+BF16 = mybir.dt.bfloat16
+I32 = mybir.dt.int32
+U32 = mybir.dt.uint32
+U16 = mybir.dt.uint16
+U8 = mybir.dt.uint8
+FP8X4 = mybir.dt.float8_e4m3fn_x4
+FP4X4 = mybir.dt.float4_e2m1fn_x4
+COPY = mybir.ActivationFunctionType.Copy
+RELU = mybir.ActivationFunctionType.Relu
+SUB = mybir.AluOpType.subtract
+
+P = 128
+PACK = 4
+LIST_ROWS = 16
+
+
+def interleave(copy, dst, src, c0, c1):
+    copy(
+        out=dst[:, c0:c1, :].rearrange("p (c i) t -> p c t i", i=4),
+        in_=src[:, :, c0:c1].rearrange("p t (c i) -> p c t i", i=4),
+    )
+
+
+def tile_picked_codes_store_one_weighedposting_outcomes_outmeet_kernel(
+    tc, ta, ga, wt_words, wt_scales, sa, sb, wb_words, wb_scales, wo_words, wo_scales, so, sp,
+    offs, offs2, offs3, offs4, offs5, offs6, offs7, out,
+):
+    nc = tc.nc
+    with ExitStack() as ctx:
+        sb_pool = ctx.enter_context(tc.tile_pool(name="keep", bufs=1))
+        shared = ctx.enter_context(tc.tile_pool(name="shared", bufs=1))
+        psum = ctx.enter_context(tc.psum_pool(name="psum", bufs=1))
+
+        def tile(name, shape, dtype):
+            return sb_pool.tile(shape, dtype, name=name, align_bytes=64)
+
+        def load_list(name, src):
+            t = tile(name, list(src.shape), U16)
+            nc.sync.dma_start(t[:], src)
+            return t
+
+        def load_rows4(name, src):
+            t = tile(name, [P, PACK], F32)
+            nc.sync.dma_start(t[:], src.rearrange("(p t) o -> p (t o)", t=PACK))
+            return t
+
+        ta_rows = ta.rearrange("(p t) c -> t p c", t=PACK)
+        ta_sb = [tile("ta%d" % t, [P, T], F32) for t in range(PACK)]
+
+        wt_plane = tile("wt_plane", [P, F], U8)
+        nc.vector.memset(wt_plane[:].bitcast(I32), 0)
+        wb_plane = tile("wb_plane", [P, N], U8)
+        wo_plane = tile("wo_plane", [P, N], U8)
+        nc.vector.memset(wb_plane[:].bitcast(I32), 0)
+        nc.vector.memset(wo_plane[:].bitcast(I32), 0)
+        board = [tile("board%d" % t, [P, C], F32) for t in range(PACK)]
+        for t in range(PACK):
+            nc.vector.memset(board[t][:], 0.0)
+
+        nc.sync.dma_start(ta_sb[0][:], ta_rows[0])
+        l1 = load_list("l1", offs)
+        ga_sb = load_rows4("ga_sb", ga)
+        nc.sync.dma_start(ta_sb[1][:], ta_rows[1])
+        wt_stage = tile("wt_stage", [4, 4, F], U8)
+        nc.sync.dma_start(
+            wt_stage[:].bitcast(I32), wt_scales[0].bitcast(I32).rearrange("(q i) c -> i q c", i=4)
+        )
+        l2 = load_list("l2", offs2)
+        for t in range(2, PACK):
+            nc.sync.dma_start(ta_sb[t][:], ta_rows[t])
+        wt_sb = tile("wt_sb", [P, F], U32)
+        nc.sync.dma_start(wt_sb[:].bitcast(I32), wt_words[0].rearrange("p c t -> p (c t)").bitcast(I32))
+        l3 = load_list("l3", offs3)
+        sa_sb = load_rows4("sa_sb", sa)
+        l4 = load_list("l4", offs4)
+        l5 = load_list("l5", offs5)
+        sb_sb = load_rows4("sb_sb", sb)
+        wb_sb = tile("wb_sb", [P, 2 * N], U8)
+        nc.sync.dma_start(wb_sb[:].bitcast(I32), wb_words[0].bitcast(I32))
+        wo_sb = tile("wo_sb", [P, N], U32)
+        nc.sync.dma_start(wo_sb[:].bitcast(I32), wo_words[0].rearrange("p c t -> p (c t)").bitcast(I32))
+        for plane, src in ((wb_plane, wb_scales), (wo_plane, wo_scales)):
+            for q in range(4):
+                nc.sync.dma_start(
+                    plane[32 * q : 32 * q + 4, :].bitcast(I32), src[0, 4 * q : 4 * q + 4, :].bitcast(I32)
+                )
+        l6 = load_list("l6", offs6)
+        l7 = load_list("l7", offs7)
+        so_sb = tile("so_sb", [P, 2], F32)
+        sp_sb = tile("sp_sb", [P, 2], F32)
+        with nc.allow_non_contiguous_dma(reason="one value a partition"):
+            nc.sync.dma_start(so_sb[:], so.rearrange("(t p) o -> p (t o)", p=P))
+            nc.sync.dma_start(sp_sb[:], sp.rearrange("(t p) o -> p (t o)", p=P))
+
+        for q in range(4):
+            nc.vector.tensor_copy(out=wt_plane[32 * q : 32 * q + 4, :].bitcast(I32), in_=wt_stage[:, q, :].bitcast(I32))
+        wg_scales = tile("wg_scales", [P, R], U8)
+        nc.vector.tensor_copy(
+            out=wg_scales[:].rearrange("p (t m) -> p m t", t=PACK), in_=wt_plane[:].indirect(l2[:])
+        )
+
+        JH = J // 2
+        xc = [tile("xc%d" % h, [P, PACK, JH], BF16) for h in range(2)]
+        for t, h in ((0, 0), (0, 1), (1, 0), (1, 1), (2, 0), (3, 0), (2, 1), (3, 1)):
+            if True:
+                cols = JH // LIST_ROWS
+                nc.scalar.activation(
+                    out=xc[h][:, t, :], in_=ta_sb[t][:].indirect(l1[:, h * cols : (h + 1) * cols]),
+                    func=COPY, scale=ga_sb[:, t : t + 1],
+                )
+        xg = [tile("xg%d" % h, [P, JH, PACK], BF16) for h in range(2)]
+        xq = [tile("xq%d" % h, [P, JH], U32) for h in range(2)]
+        xs = [tile("xs%d" % h, [P, JH], U8) for h in range(2)]
+
+        def quantize_x(h):
+            nc.vector.quantize_mx(
+                out=xq[h][:].bitcast(FP8X4), scales=xs[h][:], in_=xg[h][:].rearrange("p c t -> p (c t)")
+            )
+
+        interleave(nc.vector.tensor_copy, xg[0], xc[0], 0, JH)
+        quantize_x(0)
+        wg_words = tile("wg_words", [P, R], U32)
+        nc.vector.tensor_copy(
+            out=wg_words[:].rearrange("p (t m) -> p m t", t=PACK), in_=wt_sb[:].indirect(l2[:])
+        )
+
+        interleave(nc.scalar.copy, xg[1], xc[1], 0, JH)
+        quantize_x(1)
+
+        def product_a(t, h, dst):
+            cols = slice(t * P, (t + 1) * P)
+            nc.tensor.matmul_mx(
+                out=dst, lhsT=wg_words[:, cols].bitcast(FP8X4), lhsT_scale=wg_scales[:, cols],
+                rhs=xq[h][:].bitcast(FP8X4), rhs_scale=xs[h][:], start=True, stop=True,
+            )
+
+        a_sb = [tile("a%d" % t, [P, J], F32) for t in range(PACK - 1)]
+        a_sb.append(shared.tile([P, J], F32, name="a_last", align_bytes=64, offset=0))
+        h1 = [tile("h1_%d" % t, [P, S], F32) for t in range(PACK)]
+        h1p = [tile("h1p_%d" % t, [P, S], F32) for t in range(PACK)]
+
+        def rows_of_a(t):
+            if t < 2:
+                for h in range(2):
+                    bank = psum.tile([P, JH], F32, name="a_ps%d%d" % (t, h), tag="bank%d" % (2 * t + h))
+                    product_a(t, h, bank[:])
+                    copy = nc.scalar.copy if (t, h) == (0, 0) else nc.vector.tensor_copy
+                    copy(out=a_sb[t][:, h * JH : (h + 1) * JH], in_=bank[:])
+            else:
+                bank = psum.tile([P, J], F32, name="a_ps%d" % t, tag="bank%d" % (2 * t - 3))
+                for h in range(2):
+                    product_a(t, h, bank[:, h * JH : (h + 1) * JH])
+                nc.scalar.copy(out=a_sb[t][:], in_=bank[:])
+
+        def seats(t, s0, s1):
+            lc = slice(s0 // LIST_ROWS, s1 // LIST_ROWS)
+            nc.scalar.activation(
+                out=h1[t][:, s0:s1], in_=a_sb[t][:].indirect(l3[:, lc]), func=COPY, scale=sa_sb[:, t : t + 1]
+            )
+            if t == 0 and s0 == 0:
+                nc.vector.tensor_scalar_max(out=h1p[t][:, s0:s1], in0=h1[t][:, s0:s1], scalar1=0.0)
+            else:
+                nc.scalar.activation(out=h1p[t][:, s0:s1], in_=h1[t][:, s0:s1], func=RELU)
+            nc.vector.tensor_copy(out=board[t][:].indirect(l4[:, lc]), in_=h1p[t][:, s0:s1])
+
+        for t in range(PACK):
+            rows_of_a(t)
+            if t == 0:
+                seats(t, 0, S // 2)
+                seats(t, S // 2, S)
+            else:
+                seats(t, 0, S)
+
+        OH = O // 2
+        hid = [shared.tile([P, PACK, OH], BF16, name="hid%d" % h, align_bytes=64, offset=1024 * h) for h in range(2)]
+        for t in range(PACK):
+            for h in range(2):
+                cols = OH // LIST_ROWS
+                nc.scalar.activation(
+                    out=hid[h][:, t, :], in_=board[t][:].indirect(l5[:, h * cols : (h + 1) * cols]),
+                    func=COPY, scale=sb_sb[:, t : t + 1],
+                )
+        hg = [tile("hg%d" % h, [P, OH, PACK], BF16) for h in range(2)]
+        hq = [tile("hq%d" % h, [P, OH], U32) for h in range(2)]
+        hs = [tile("hs%d" % h, [P, OH], U8) for h in range(2)]
+        for h in range(2):
+            interleave(nc.vector.tensor_copy, hg[h], hid[h], 0, OH)
+        for h in range(2):
+            nc.vector.quantize_mx(
+                out=hq[h][:].bitcast(FP8X4), scales=hs[h][:], in_=hg[h][:].rearrange("p c t -> p (c t)")
+            )
+
+        pq_ps = {}
+        for nt in range(2):
+            for h in range(2):
+                for w in range(2):
+                    i = 2 * nt + w
+                    bank = psum.tile([P, OH], F32, name="pq_ps%d%d" % (i, h), tag="bank%d" % (4 * h + i))
+                    pq_ps[i, h] = bank
+                    cols = slice(nt * P, (nt + 1) * P)
+                    if w == 0:
+                        lhsT = wb_sb[:, 2 * nt * P : 2 * (nt + 1) * P].bitcast(FP4X4)
+                        plane = wb_plane
+                    else:
+                        lhsT = wo_sb[:, cols].bitcast(FP8X4)
+                        plane = wo_plane
+                    nc.tensor.matmul_mx(
+                        out=bank[:], lhsT=lhsT, lhsT_scale=plane[:, cols],
+                        rhs=hq[h][:].bitcast(FP8X4), rhs_scale=hs[h][:], start=True, stop=True,
+                    )
+        pq_sb = [tile("pq%d" % i, [P, O], F32) for i in range(4)]
+        for nt, h, w in [(nt, h, w) for nt in range(2) for h in range(2) for w in range(2)]:
+            if True:
+                i = 2 * nt + w
+                dst = pq_sb[i][:, h * OH : (h + 1) * OH]
+                if h == 0 and nt == 0:
+                    nc.scalar.copy(out=dst, in_=pq_ps[i, h][:])
+                else:
+                    nc.vector.tensor_copy(out=dst, in_=pq_ps[i, h][:])
+        picked = [tile("picked%d" % i, [P, U], F32) for i in range(4)]
+        for nt in range(2):
+            for w, (lst, weight) in enumerate(((l6, so_sb), (l7, sp_sb))):
+                i = 2 * nt + w
+                nc.scalar.activation(
+                    out=picked[i][:], in_=pq_sb[i][:].indirect(lst[:]), func=COPY, scale=weight[:, nt : nt + 1]
+                )
+            y = tile("y%d" % nt, [P, U], F32)
+            nc.vector.tensor_tensor(out=y[:], in0=picked[2 * nt][:], in1=picked[2 * nt + 1][:], op=SUB)
+            nc.sync.dma_start(out[nt * P : (nt + 1) * P, :], y[:])

@@ -55,6 +55,11 @@ def tile_picked_codes_store_one_weighedposting_outcomes_outmeet_kernel(
         ta_rows = ta.rearrange("(p t) c -> t p c", t=PACK)
         ta_sb = [tile("ta%d" % t, [P, T], F32) for t in range(PACK)]
 
+        warm_in = tile("warm_in", [P, 1], F32)
+        warm_out = tile("warm_out", [P, 1], F32)
+        nc.vector.memset(warm_in[:], 0.0)
+        nc.scalar.activation(out=warm_out[:], in_=warm_in[:], func=COPY)
+
         wt_plane = tile("wt_plane", [P, F], U8)
         nc.vector.memset(wt_plane[:].bitcast(I32), 0)
         wb_plane = tile("wb_plane", [P, N], U8)

@@ -74,10 +74,12 @@ def tile_picked_codes_store_one_weighedposting_outcomes_outmeet_kernel(
         l1 = load_list("l1", offs)
         ga_sb = load_rows4("ga_sb", ga)
         nc.sync.dma_start(ta_sb[1][:], ta_rows[1])
-        wt_stage = tile("wt_stage", [4, 4, F], U8)
-        nc.sync.dma_start(
-            wt_stage[:].bitcast(I32), wt_scales[0].bitcast(I32).rearrange("(q i) c -> i q c", i=4)
-        )
+        wt_stage = tile("wt_stage", [P, 2, F], U8)
+        for half in range(2):
+            nc.sync.dma_start(
+                wt_stage[64 * half : 64 * half + 4].bitcast(I32),
+                wt_scales[0, 8 * half : 8 * half + 8].bitcast(I32).rearrange("(q i) c -> i q c", i=4),
+            )
         l2 = load_list("l2", offs2)
         for t in range(2, PACK):
             nc.sync.dma_start(ta_sb[t][:], ta_rows[t])
@@ -106,7 +108,7 @@ def tile_picked_codes_store_one_weighedposting_outcomes_outmeet_kernel(
             nc.sync.dma_start(sp_sb[:], sp.rearrange("(t p) o -> p (t o)", p=P))
 
         for q in range(4):
-            nc.vector.tensor_copy(out=wt_plane[32 * q : 32 * q + 4, :].bitcast(I32), in_=wt_stage[:, q, :].bitcast(I32))
+            nc.vector.tensor_copy(out=wt_plane[32 * q : 32 * q + 4, :].bitcast(I32), in_=wt_stage[64 * (q // 2) : 64 * (q // 2) + 4, q % 2, :].bitcast(I32))
         wg_scales = tile("wg_scales", [P, R], U8)
         nc.vector.tensor_copy(
             out=wg_scales[:].rearrange("p (t m) -> p m t", t=PACK), in_=wt_plane[:].indirect(l2[:])
@@ -122,12 +124,13 @@ def tile_picked_codes_store_one_weighedposting_outcomes_outmeet_kernel(
                     func=COPY, scale=ga_sb[:, t : t + 1],
                 )
         xg = [tile("xg%d" % h, [P, JH, PACK], BF16) for h in range(2)]
-        xq = [tile("xq%d" % h, [P, JH], U32) for h in range(2)]
-        xs = [tile("xs%d" % h, [P, JH], U8) for h in range(2)]
+        xq = tile("xq", [P, J], U32)
+        xs = tile("xs", [P, J], U8)
 
         def quantize_x(h):
+            cols = slice(h * JH, (h + 1) * JH)
             nc.vector.quantize_mx(
-                out=xq[h][:].bitcast(FP8X4), scales=xs[h][:], in_=xg[h][:].rearrange("p c t -> p (c t)")
+                out=xq[:, cols].bitcast(FP8X4), scales=xs[:, cols], in_=xg[h][:].rearrange("p c t -> p (c t)")
             )
 
         interleave(nc.vector.tensor_copy, xg[0], xc[0], 0, JH)
@@ -140,49 +143,42 @@ def tile_picked_codes_store_one_weighedposting_outcomes_outmeet_kernel(
         interleave(nc.scalar.copy, xg[1], xc[1], 0, JH)
         quantize_x(1)
 
-        def product_a(t, h, dst):
+        def product_a(t, slots, dst):
             cols = slice(t * P, (t + 1) * P)
             nc.tensor.matmul_mx(
                 out=dst, lhsT=wg_words[:, cols].bitcast(FP8X4), lhsT_scale=wg_scales[:, cols],
-                rhs=xq[h][:].bitcast(FP8X4), rhs_scale=xs[h][:], start=True, stop=True,
+                rhs=xq[:, slots].bitcast(FP8X4), rhs_scale=xs[:, slots], start=True, stop=True,
             )
 
         a_sb = [tile("a%d" % t, [P, J], F32) for t in range(PACK - 1)]
         a_sb.append(shared.tile([P, J], F32, name="a_last", align_bytes=64, offset=0))
         h1 = [tile("h1_%d" % t, [P, S], F32) for t in range(PACK)]
-        h1p = [tile("h1p_%d" % t, [P, S], F32) for t in range(PACK)]
-
-        def rows_of_a(t):
-            if t < 2:
-                for h in range(2):
-                    bank = psum.tile([P, JH], F32, name="a_ps%d%d" % (t, h), tag="bank%d" % (2 * t + h))
-                    product_a(t, h, bank[:])
-                    copy = nc.scalar.copy if (t, h) == (0, 0) else nc.vector.tensor_copy
-                    copy(out=a_sb[t][:, h * JH : (h + 1) * JH], in_=bank[:])
-            else:
-                bank = psum.tile([P, J], F32, name="a_ps%d" % t, tag="bank%d" % (2 * t - 3))
-                for h in range(2):
-                    product_a(t, h, bank[:, h * JH : (h + 1) * JH])
-                nc.scalar.copy(out=a_sb[t][:], in_=bank[:])
-
-        def seats(t, s0, s1):
-            lc = slice(s0 // LIST_ROWS, s1 // LIST_ROWS)
-            nc.scalar.activation(
-                out=h1[t][:, s0:s1], in_=a_sb[t][:].indirect(l3[:, lc]), func=COPY, scale=sa_sb[:, t : t + 1]
-            )
-            if t == 0 and s0 == 0:
-                nc.vector.tensor_scalar_max(out=h1p[t][:, s0:s1], in0=h1[t][:, s0:s1], scalar1=0.0)
-            else:
-                nc.scalar.activation(out=h1p[t][:, s0:s1], in_=h1[t][:, s0:s1], func=RELU)
-            nc.vector.tensor_copy(out=board[t][:].indirect(l4[:, lc]), in_=h1p[t][:, s0:s1])
 
         for t in range(PACK):
-            rows_of_a(t)
             if t == 0:
-                seats(t, 0, S // 2)
-                seats(t, S // 2, S)
+                for h, copy in enumerate((nc.scalar.copy, nc.vector.tensor_copy)):
+                    slots = slice(h * JH, (h + 1) * JH)
+                    bank = psum.tile([P, JH], F32, name="a_ps0%d" % h, tag="bank%d" % h)
+                    product_a(t, slots, bank[:])
+                    copy(out=a_sb[t][:, slots], in_=bank[:])
             else:
-                seats(t, 0, S)
+                bank = psum.tile([P, J], F32, name="a_ps%d" % t, tag="bank%d" % (t + 1))
+                product_a(t, slice(0, J), bank[:])
+                copy = nc.vector.tensor_copy if t == 1 else nc.scalar.copy
+                copy(out=a_sb[t][:], in_=bank[:])
+            nc.scalar.activation(out=h1[t][:], in_=a_sb[t][:].indirect(l3[:]), func=COPY, scale=sa_sb[:, t : t + 1])
+            seats = h1[t]
+            if t >= 2:
+                seats = tile("h1p_%d" % t, [P, S], F32)
+                nc.scalar.activation(out=seats[:], in_=h1[t][:], func=RELU)
+            nc.vector.tensor_copy(out=board[t][:].indirect(l4[:]), in_=seats[:])
+
+        g1 = []
+        for t, tag in enumerate(("a2", "h1_3")):
+            kept = sb_pool.tile([P, C], F32, name="g1_%d" % t, tag=tag, align_bytes=64)
+            nc.scalar.activation(out=kept[:], in_=board[t][:], func=RELU)
+            g1.append(kept)
+        g1 += board[2:]
 
         OH = O // 2
         hid = [shared.tile([P, PACK, OH], BF16, name="hid%d" % h, align_bytes=64, offset=1024 * h) for h in range(2)]
@@ -190,46 +186,40 @@ def tile_picked_codes_store_one_weighedposting_outcomes_outmeet_kernel(
             for h in range(2):
                 cols = OH // LIST_ROWS
                 nc.scalar.activation(
-                    out=hid[h][:, t, :], in_=board[t][:].indirect(l5[:, h * cols : (h + 1) * cols]),
+                    out=hid[h][:, t, :], in_=g1[t][:].indirect(l5[:, h * cols : (h + 1) * cols]),
                     func=COPY, scale=sb_sb[:, t : t + 1],
                 )
         hg = [tile("hg%d" % h, [P, OH, PACK], BF16) for h in range(2)]
-        hq = [tile("hq%d" % h, [P, OH], U32) for h in range(2)]
-        hs = [tile("hs%d" % h, [P, OH], U8) for h in range(2)]
+        hq = tile("hq", [P, O], U32)
+        hs = tile("hs", [P, O], U8)
         for h in range(2):
             interleave(nc.vector.tensor_copy, hg[h], hid[h], 0, OH)
         for h in range(2):
+            cols = slice(h * OH, (h + 1) * OH)
             nc.vector.quantize_mx(
-                out=hq[h][:].bitcast(FP8X4), scales=hs[h][:], in_=hg[h][:].rearrange("p c t -> p (c t)")
+                out=hq[:, cols].bitcast(FP8X4), scales=hs[:, cols], in_=hg[h][:].rearrange("p c t -> p (c t)")
             )
 
-        pq_ps = {}
-        for nt in range(2):
-            for h in range(2):
-                for w in range(2):
-                    i = 2 * nt + w
-                    bank = psum.tile([P, OH], F32, name="pq_ps%d%d" % (i, h), tag="bank%d" % (4 * h + i))
-                    pq_ps[i, h] = bank
-                    cols = slice(nt * P, (nt + 1) * P)
-                    if w == 0:
-                        lhsT = wb_sb[:, 2 * nt * P : 2 * (nt + 1) * P].bitcast(FP4X4)
-                        plane = wb_plane
-                    else:
-                        lhsT = wo_sb[:, cols].bitcast(FP8X4)
-                        plane = wo_plane
-                    nc.tensor.matmul_mx(
-                        out=bank[:], lhsT=lhsT, lhsT_scale=plane[:, cols],
-                        rhs=hq[h][:].bitcast(FP8X4), rhs_scale=hs[h][:], start=True, stop=True,
-                    )
         pq_sb = [tile("pq%d" % i, [P, O], F32) for i in range(4)]
-        for nt, h, w in [(nt, h, w) for nt in range(2) for h in range(2) for w in range(2)]:
-            if True:
-                i = 2 * nt + w
-                dst = pq_sb[i][:, h * OH : (h + 1) * OH]
-                if h == 0 and nt == 0:
-                    nc.scalar.copy(out=dst, in_=pq_ps[i, h][:])
-                else:
-                    nc.vector.tensor_copy(out=dst, in_=pq_ps[i, h][:])
+
+        def outcome(nt, w, places, bank_no, copy):
+            cols = slice(nt * P, (nt + 1) * P)
+            if w == 0:
+                lhsT, plane = wb_sb[:, 2 * nt * P : 2 * (nt + 1) * P].bitcast(FP4X4), wb_plane
+            else:
+                lhsT, plane = wo_sb[:, cols].bitcast(FP8X4), wo_plane
+            bank = psum.tile([P, places.stop - places.start], F32, name="pq_ps%d" % bank_no, tag="bank%d" % bank_no)
+            nc.tensor.matmul_mx(
+                out=bank[:], lhsT=lhsT, lhsT_scale=plane[:, cols],
+                rhs=hq[:, places].bitcast(FP8X4), rhs_scale=hs[:, places], start=True, stop=True,
+            )
+            copy(out=pq_sb[2 * nt + w][:, places], in_=bank[:])
+
+        for h, copy in enumerate((nc.scalar.copy, nc.vector.tensor_copy)):
+            for w in range(2):
+                outcome(0, w, slice(h * OH, (h + 1) * OH), 2 * h + w, copy)
+        for w in range(2):
+            outcome(1, w, slice(0, O), 4 + w, nc.vector.tensor_copy)
         picked = [tile("picked%d" % i, [P, U], F32) for i in range(4)]
         for nt in range(2):
             for w, (lst, weight) in enumerate(((l6, so_sb), (l7, sp_sb))):

from contextlib import ExitStack

import concourse.mybir as mybir

K, J, R, T, F, O, C, S, N, U = 512, 512, 512, 1024, 1024, 256, 512, 256, 256, 128
FLOPS = 2 * K * R * J + 2 * 2 * R * N * O

F32 = mybir.dt.float32
BF16 = mybir.dt.bfloat16
I32 = mybir.dt.int32
U32 = mybir.dt.uint32
U16 = mybir.dt.uint16
U8 = mybir.dt.uint8
FP8X4 = mybir.dt.float8_e4m3fn_x4
FP4X4 = mybir.dt.float4_e2m1fn_x4
COPY = mybir.ActivationFunctionType.Copy
RELU = mybir.ActivationFunctionType.Relu
SUB = mybir.AluOpType.subtract

P = 128
PACK = 4
LIST_ROWS = 16


def interleave(copy, dst, src, c0, c1):
    copy(
        out=dst[:, c0:c1, :].rearrange("p (c i) t -> p c t i", i=4),
        in_=src[:, :, c0:c1].rearrange("p t (c i) -> p c t i", i=4),
    )


def tile_picked_codes_store_one_weighedposting_outcomes_outmeet_kernel(
    tc, ta, ga, wt_words, wt_scales, sa, sb, wb_words, wb_scales, wo_words, wo_scales, so, sp,
    offs, offs2, offs3, offs4, offs5, offs6, offs7, out,
):
    nc = tc.nc
    with ExitStack() as ctx:
        sb_pool = ctx.enter_context(tc.tile_pool(name="keep", bufs=1))
        shared = ctx.enter_context(tc.tile_pool(name="shared", bufs=1))
        psum = ctx.enter_context(tc.psum_pool(name="psum", bufs=1))

        def tile(name, shape, dtype):
            return sb_pool.tile(shape, dtype, name=name, align_bytes=64)

        def load_list(name, src):
            t = tile(name, list(src.shape), U16)
            nc.sync.dma_start(t[:], src)
            return t

        def load_rows4(name, src):
            t = tile(name, [P, PACK], F32)
            nc.sync.dma_start(t[:], src.rearrange("(p t) o -> p (t o)", t=PACK))
            return t

        ta_rows = ta.rearrange("(p t) c -> t p c", t=PACK)
        ta_sb = [tile("ta%d" % t, [P, T], F32) for t in range(PACK)]

        warm_in = tile("warm_in", [P, 1], F32)
        warm_out = tile("warm_out", [P, 1], F32)
        nc.vector.memset(warm_in[:], 0.0)
        nc.scalar.activation(out=warm_out[:], in_=warm_in[:], func=COPY)

        wt_plane = tile("wt_plane", [P, F], U8)
        nc.vector.memset(wt_plane[:].bitcast(I32), 0)
        wb_plane = tile("wb_plane", [P, N], U8)
        wo_plane = tile("wo_plane", [P, N], U8)
        nc.vector.memset(wb_plane[:].bitcast(I32), 0)
        nc.vector.memset(wo_plane[:].bitcast(I32), 0)
        board = [tile("board%d" % t, [P, C], F32) for t in range(PACK)]
        for t in range(PACK):
            nc.vector.memset(board[t][:], 0.0)

        nc.sync.dma_start(ta_sb[0][:], ta_rows[0])
        l1 = load_list("l1", offs)
        ga_sb = load_rows4("ga_sb", ga)
        nc.sync.dma_start(ta_sb[1][:], ta_rows[1])
        wt_stage = tile("wt_stage", [P, 2, F], U8)
        for half in range(2):
            nc.sync.dma_start(
                wt_stage[64 * half : 64 * half + 4].bitcast(I32),
                wt_scales[0, 8 * half : 8 * half + 8].bitcast(I32).rearrange("(q i) c -> i q c", i=4),
            )
        l2 = load_list("l2", offs2)
        for t in range(2, PACK):
            nc.sync.dma_start(ta_sb[t][:], ta_rows[t])
        wt_sb = tile("wt_sb", [P, F], U32)
        nc.sync.dma_start(wt_sb[:].bitcast(I32), wt_words[0].rearrange("p c t -> p (c t)").bitcast(I32))
        l3 = load_list("l3", offs3)
        sa_sb = load_rows4("sa_sb", sa)
        l4 = load_list("l4", offs4)
        l5 = load_list("l5", offs5)
        sb_sb = load_rows4("sb_sb", sb)
        wb_sb = tile("wb_sb", [P, 2 * N], U8)
        nc.sync.dma_start(wb_sb[:].bitcast(I32), wb_words[0].bitcast(I32))
        wo_sb = tile("wo_sb", [P, N], U32)
        nc.sync.dma_start(wo_sb[:].bitcast(I32), wo_words[0].rearrange("p c t -> p (c t)").bitcast(I32))
        for plane, src in ((wb_plane, wb_scales), (wo_plane, wo_scales)):
            for q in range(4):
                nc.sync.dma_start(
                    plane[32 * q : 32 * q + 4, :].bitcast(I32), src[0, 4 * q : 4 * q + 4, :].bitcast(I32)
                )
        l6 = load_list("l6", offs6)
        l7 = load_list("l7", offs7)
        so_sb = tile("so_sb", [P, 2], F32)
        sp_sb = tile("sp_sb", [P, 2], F32)
        with nc.allow_non_contiguous_dma(reason="one value a partition"):
            nc.sync.dma_start(so_sb[:], so.rearrange("(t p) o -> p (t o)", p=P))
            nc.sync.dma_start(sp_sb[:], sp.rearrange("(t p) o -> p (t o)", p=P))

        for q in range(4):
            nc.vector.tensor_copy(out=wt_plane[32 * q : 32 * q + 4, :].bitcast(I32), in_=wt_stage[64 * (q // 2) : 64 * (q // 2) + 4, q % 2, :].bitcast(I32))
        wg_scales = tile("wg_scales", [P, R], U8)
        nc.vector.tensor_copy(
            out=wg_scales[:].rearrange("p (t m) -> p m t", t=PACK), in_=wt_plane[:].indirect(l2[:])
        )

        JH = J // 2
        xc = [tile("xc%d" % h, [P, PACK, JH], BF16) for h in range(2)]
        for t, h in ((0, 0), (0, 1), (1, 0), (1, 1), (2, 0), (3, 0), (2, 1), (3, 1)):
            if True:
                cols = JH // LIST_ROWS
                nc.scalar.activation(
                    out=xc[h][:, t, :], in_=ta_sb[t][:].indirect(l1[:, h * cols : (h + 1) * cols]),
                    func=COPY, scale=ga_sb[:, t : t + 1],
                )
        xg = [tile("xg%d" % h, [P, JH, PACK], BF16) for h in range(2)]
        xq = tile("xq", [P, J], U32)
        xs = tile("xs", [P, J], U8)

        def quantize_x(h):
            cols = slice(h * JH, (h + 1) * JH)
            nc.vector.quantize_mx(
                out=xq[:, cols].bitcast(FP8X4), scales=xs[:, cols], in_=xg[h][:].rearrange("p c t -> p (c t)")
            )

        interleave(nc.vector.tensor_copy, xg[0], xc[0], 0, JH)
        quantize_x(0)
        wg_words = tile("wg_words", [P, R], U32)
        nc.vector.tensor_copy(
            out=wg_words[:].rearrange("p (t m) -> p m t", t=PACK), in_=wt_sb[:].indirect(l2[:])
        )

        interleave(nc.scalar.copy, xg[1], xc[1], 0, JH)
        quantize_x(1)

        def product_a(t, slots, dst):
            cols = slice(t * P, (t + 1) * P)
            nc.tensor.matmul_mx(
                out=dst, lhsT=wg_words[:, cols].bitcast(FP8X4), lhsT_scale=wg_scales[:, cols],
                rhs=xq[:, slots].bitcast(FP8X4), rhs_scale=xs[:, slots], start=True, stop=True,
            )

        a_sb = [tile("a%d" % t, [P, J], F32) for t in range(PACK - 1)]
        a_sb.append(shared.tile([P, J], F32, name="a_last", align_bytes=64, offset=0))
        h1 = [tile("h1_%d" % t, [P, S], F32) for t in range(PACK)]

        for t in range(PACK):
            if t == 0:
                for h, copy in enumerate((nc.scalar.copy, nc.vector.tensor_copy)):
                    slots = slice(h * JH, (h + 1) * JH)
                    bank = psum.tile([P, JH], F32, name="a_ps0%d" % h, tag="bank%d" % h)
                    product_a(t, slots, bank[:])
                    copy(out=a_sb[t][:, slots], in_=bank[:])
            else:
                bank = psum.tile([P, J], F32, name="a_ps%d" % t, tag="bank%d" % (t + 1))
                product_a(t, slice(0, J), bank[:])
                copy = nc.vector.tensor_copy if t == 1 else nc.scalar.copy
                copy(out=a_sb[t][:], in_=bank[:])
            nc.scalar.activation(out=h1[t][:], in_=a_sb[t][:].indirect(l3[:]), func=COPY, scale=sa_sb[:, t : t + 1])
            seats = h1[t]
            if t >= 2:
                seats = tile("h1p_%d" % t, [P, S], F32)
                nc.scalar.activation(out=seats[:], in_=h1[t][:], func=RELU)
            nc.vector.tensor_copy(out=board[t][:].indirect(l4[:]), in_=seats[:])

        g1 = []
        for t, tag in enumerate(("a2", "h1_3")):
            kept = sb_pool.tile([P, C], F32, name="g1_%d" % t, tag=tag, align_bytes=64)
            nc.scalar.activation(out=kept[:], in_=board[t][:], func=RELU)
            g1.append(kept)
        g1 += board[2:]

        OH = O // 2
        hid = [shared.tile([P, PACK, OH], BF16, name="hid%d" % h, align_bytes=64, offset=1024 * h) for h in range(2)]
        for t in range(PACK):
            for h in range(2):
                cols = OH // LIST_ROWS
                nc.scalar.activation(
                    out=hid[h][:, t, :], in_=g1[t][:].indirect(l5[:, h * cols : (h + 1) * cols]),
                    func=COPY, scale=sb_sb[:, t : t + 1],
                )
        hg = [tile("hg%d" % h, [P, OH, PACK], BF16) for h in range(2)]
        hq = tile("hq", [P, O], U32)
        hs = tile("hs", [P, O], U8)
        for h in range(2):
            interleave(nc.vector.tensor_copy, hg[h], hid[h], 0, OH)
        for h in range(2):
            cols = slice(h * OH, (h + 1) * OH)
            nc.vector.quantize_mx(
                out=hq[:, cols].bitcast(FP8X4), scales=hs[:, cols], in_=hg[h][:].rearrange("p c t -> p (c t)")
            )

        pq_sb = [tile("pq%d" % i, [P, O], F32) for i in range(4)]

        def outcome(nt, w, places, bank_no, copy):
            cols = slice(nt * P, (nt + 1) * P)
            if w == 0:
                lhsT, plane = wb_sb[:, 2 * nt * P : 2 * (nt + 1) * P].bitcast(FP4X4), wb_plane
            else:
                lhsT, plane = wo_sb[:, cols].bitcast(FP8X4), wo_plane
            bank = psum.tile([P, places.stop - places.start], F32, name="pq_ps%d" % bank_no, tag="bank%d" % bank_no)
            nc.tensor.matmul_mx(
                out=bank[:], lhsT=lhsT, lhsT_scale=plane[:, cols],
                rhs=hq[:, places].bitcast(FP8X4), rhs_scale=hs[:, places], start=True, stop=True,
            )
            copy(out=pq_sb[2 * nt + w][:, places], in_=bank[:])

        for h, copy in enumerate((nc.scalar.copy, nc.vector.tensor_copy)):
            for w in range(2):
                outcome(0, w, slice(h * OH, (h + 1) * OH), 2 * h + w, copy)
        for w in range(2):
            outcome(1, w, slice(0, O), 4 + w, nc.vector.tensor_copy)
        picked = [tile("picked%d" % i, [P, U], F32) for i in range(4)]
        for nt in range(2):
            for w, (lst, weight) in enumerate(((l6, so_sb), (l7, sp_sb))):
                i = 2 * nt + w
                nc.scalar.activation(
                    out=picked[i][:], in_=pq_sb[i][:].indirect(lst[:]), func=COPY, scale=weight[:, nt : nt + 1]
                )
            y = tile("y%d" % nt, [P, U], F32)
            nc.vector.tensor_tensor(out=y[:], in0=picked[2 * nt][:], in1=picked[2 * nt + 1][:], op=SUB)
            nc.sync.dma_start(out[nt * P : (nt + 1) * P, :], y[:])
